import numpy as np
import ml_dtypes


def mxq(x, axis, fmt="e4m3"):
    dtype, down = {"e4m3": (ml_dtypes.float8_e4m3fn, 7), "e5m2": (ml_dtypes.float8_e5m2, 14)}[fmt]
    v = np.moveaxis(np.asarray(x, np.float32).astype(ml_dtypes.bfloat16).astype(np.float64), axis, -1)
    blocks = v.reshape(v.shape[:-1] + (-1, 32))
    amax = np.abs(blocks).max(-1, keepdims=True)
    byte = np.maximum(np.where(amax > 0, np.frexp(amax)[1] - 1 + 127, 0) - down, 1)
    scale = np.exp2(byte - 127.0)
    codes = (blocks / scale).astype(np.float32).astype(dtype).astype(np.float64)
    return np.moveaxis((codes * scale).reshape(v.shape), -1, axis)


WIDE = False


def mx_kscale(k):
    if not WIDE:
        return np.ones(k)
    levels = np.array([10, -10, 5, -5, 0])
    if k % 512:
        return np.exp2(np.random.permutation(np.resize(levels, k // 32))).repeat(32)
    a = np.empty((k // 512, 16))
    for p in range(k // 512):
        a[p, :8] = np.random.permutation(np.resize(levels, 8))
        for g in range(8):
            far = levels[np.abs(levels - a[p, g]) >= 10]
            a[p, g + 8] = far[np.random.randint(len(far))]
    return np.exp2(a.ravel()).repeat(32)


def f64(x):
    return np.asarray(x).astype(np.float64)


def striped8(idx):
    return np.asarray(idx).reshape(8, -1, 16).transpose(0, 2, 1).reshape(128, -1).astype(np.uint16)


def unstriped8(offs):
    return offs.reshape(8, 16, -1).transpose(0, 2, 1).reshape(8, -1).astype(np.int64)


def pick8(x, idx, run):
    r = np.arange(len(x))
    return x[r[:, None], idx[r % (8 * run) // run]]


def rot(x):
    y = x.reshape(-1, 2, x.shape[1])
    return np.stack([-y[:, 1], y[:, 0]], axis=1).reshape(x.shape)


D, T, I, Q, X, E, U = 512, 1024, 512, 256, 32, 512, 1024


def setup_inputs():
    n = np.random.standard_normal
    idx = np.stack([np.random.permutation(T)[:I] for _ in range(8)])
    idx2 = np.stack([np.random.randint(0, U, I) for _ in range(8)])
    fd = mx_kscale(D)
    fi = mx_kscale(I)
    ti = np.ones((8, T))
    np.put_along_axis(ti, idx, np.tile(fi, (8, 1)), axis=1)
    return {
        "query": (n((D, Q)) * (np.arange(D)[:, None] // 64 == np.arange(Q) % 8) * 0.0625 * fd[:, None]).astype(np.float32),
        "keys": (n((D, T)) / fd[:, None]).astype(np.float32),
        "cosn": (np.repeat(np.round(np.cos(np.arange(D // 2)[:, None] * 0.11 + np.arange(U)[None] * 0.37) * 64) / 64, 2, axis=0)).astype(np.float32),
        "sinn": (np.repeat(np.round(np.sin(np.arange(D // 2)[:, None] * 0.11 + np.arange(U)[None] * 0.37) * 64) / 64, 2, axis=0)).astype(np.float32),
        "size": (np.random.uniform(0.5, 2.0, (1, I)) * fi).astype(np.float32),
        "vals": (n((E, T)) / ti[np.arange(E) % 512 // 64]).astype(np.float32),
        "own": ((np.arange(E)[:, None] // 64 == np.arange(Q) % 8) * 1.0).astype(np.float32),
        "offs": striped8(idx),
        "offs2": striped8(idx2),
    }


def reference(query, keys, cosn, sinn, size, vals, own, offs, offs2):
    idx = unstriped8(offs)
    idx2 = unstriped8(offs2)
    kr = rot(pick8(f64(keys), idx, 64))
    km = pick8(f64(keys), idx, 64) * pick8(f64(cosn), idx2, 64) + kr * pick8(f64(sinn), idx2, 64)
    queryq = mxq(f64(query), 0, "e4m3")
    kmq = mxq(km, 0, "e4m3")
    a = queryq.T @ kmq
    p = np.exp(a - np.max(a, axis=1, keepdims=True))
    w = p * f64(size) / np.sum(p, axis=1, keepdims=True)
    wt = w.T
    vt = pick8(f64(vals), idx, 64).T
    vtq = mxq(vt, 0, "e4m3")
    wtq = mxq(wt, 0, "e4m3")
    o = vtq.T @ wtq
    ob = o * f64(own)
    y = ob.reshape(E, X, Q // X).sum(axis=2)
    return y

@@ -1,0 +1,233 @@
+from contextlib import ExitStack
+
+import concourse.mybir as mybir
+from concourse.masks import make_identity
+
+F32 = mybir.dt.float32
+BF16 = mybir.dt.bfloat16
+U32 = mybir.dt.uint32
+U16 = mybir.dt.uint16
+U8 = mybir.dt.uint8
+FP8X4 = mybir.dt.float8_e4m3fn_x4
+ALU = mybir.AluOpType
+ACT = mybir.ActivationFunctionType
+AX = mybir.AxisListType
+
+P = 128
+PACK = 4
+D, T, I, Q, X, E = 512, 1024, 512, 256, 32, 512
+HEADS = Q // X
+FLOPS = 2 * D * Q * I + 2 * I * E * Q
+BYTES = 4 * (D * Q + D * T + D * T + I + E * T + E * Q + E * X) + 2 * 2 * P * (I // 16)
+
+
+def tile_attend_ownlists_rope_kernel(tc, query, keys, cosn, sinn, size, vals, own, offs, offs2, out):
+    nc = tc.nc
+    with ExitStack() as ctx:
+        sb = ctx.enter_context(tc.tile_pool(name="sb", bufs=1))
+        ps = ctx.enter_context(tc.psum_pool(name="ps", bufs=1))
+
+        def plane(src, t):
+            return src.rearrange("(p t) c -> p t c", t=PACK)[:, t, :]
+
+        tok = sb.tile([P, I // 16], U16, name="tok")
+        pos = sb.tile([P, I // 16], U16, name="pos")
+        k_win = [sb.tile([P, T], F32, name="k_win%d" % t) for t in range(PACK)]
+        c_win = [sb.tile([P, T], F32, name="c_win%d" % g) for g in range(2)]
+        s_win = [sb.tile([P, T], F32, name="s_win%d" % g) for g in range(2)]
+        v_raw = [sb.tile([P, T], F32, name="v_raw%d" % t) for t in range(PACK)]
+        q_raw = sb.tile([P, PACK * Q], F32, name="q_raw")
+        own_sb = sb.tile([P, PACK * Q], F32, name="own_sb")
+        size_col = sb.tile([P, PACK], F32, name="size_col")
+
+        def load(dst, src):
+            nc.sync.dma_start(out=dst, in_=src)
+
+        load(k_win[0][:], plane(keys, 0))
+        load(tok[:], offs)
+        load(c_win[0][:], plane(cosn, 0))
+        load(pos[:], offs2)
+        load(k_win[1][:], plane(keys, 1))
+        load(s_win[0][:], plane(sinn, 0))
+        load(v_raw[0][:], plane(vals, 0))
+        load(v_raw[1][:], plane(vals, 1))
+        load(k_win[2][:], plane(keys, 2))
+        load(c_win[1][:], plane(cosn, 2))
+        load(k_win[3][:], plane(keys, 3))
+        load(s_win[1][:], plane(sinn, 2))
+        load(q_raw[:], query.rearrange("(p t) q -> p (t q)", t=PACK))
+        load(v_raw[2][:], plane(vals, 2))
+        load(v_raw[3][:], plane(vals, 3))
+        load(size_col[:], size.rearrange("o (s r) -> (o s) r", r=PACK))
+        load(own_sb[:], own.rearrange("(p t) q -> p (t q)", t=PACK))
+
+        ident = sb.tile([P, P], F32, name="ident")
+        make_identity(nc, ident[:])
+
+        cos_terms = sb.tile([P, PACK * I], F32, name="cos_terms", tag="hold0", align_bytes=64)
+        sin_terms = sb.tile([P, PACK * I], F32, name="sin_terms")
+
+        def cols(t, n=1):
+            return slice(t * I, (t + n) * I)
+
+        def rope_pair(g):
+            kg = sb.tile([P, 2 * I], F32, name="kg%d" % g)
+            cg = sb.tile([P, I], F32, name="cg%d" % g)
+            sg = sb.tile([P, I], F32, name="sg%d" % g)
+            nc.vector.tensor_copy(kg[:, cols(0)], k_win[2 * g][:].indirect(tok[:]))
+            nc.vector.tensor_copy(cg[:], c_win[g][:].indirect(pos[:]))
+            nc.vector.tensor_copy(kg[:, cols(1)], k_win[2 * g + 1][:].indirect(tok[:]))
+            nc.vector.tensor_copy(sg[:], s_win[g][:].indirect(pos[:]))
+            nc.vector.tensor_tensor(
+                cos_terms[:, cols(2 * g, 2)].rearrange("p (t i) -> p t i", t=2),
+                kg[:].rearrange("p (t i) -> p t i", t=2),
+                cg[:].unsqueeze(1).to_broadcast([P, 2, I]),
+                ALU.mult,
+            )
+            nc.vector.scalar_tensor_tensor(sin_terms[:, cols(2 * g)], kg[:, cols(1)], -1.0, sg[:], ALU.mult, ALU.mult)
+            nc.vector.tensor_tensor(sin_terms[:, cols(2 * g + 1)], kg[:, cols(0)], sg[:], ALU.mult)
+
+        v_gath = []
+
+        def gather_vals(t):
+            v_win = sb.tile([P, T], BF16, name="v_win%d" % t)
+            vg = sb.tile([P, I], BF16, name="vg%d" % t)
+            nc.scalar.activation(v_win[:], v_raw[t][:], ACT.Copy)
+            nc.scalar.activation(vg[:], v_win[:].indirect(tok[:]), ACT.Copy)
+            v_gath.append(vg)
+
+        v_codes, v_scales = [], []
+        v_grouped = []
+
+        def turn_vals(h):
+            bank = ps.tile([P, 4 * P], F32, name="vt_bank%d" % h, tag="vo%d" % h)
+            for j in range(2):
+                words = v_gath[2 * h + j][:].bitcast(F32)
+                for u in range(2):
+                    nc.tensor.transpose(bank[:, (2 * j + u) * P : (2 * j + u + 1) * P], words[:, u : I // 2 : 2], ident[:])
+            grouped = sb.tile([P, 2 * P * PACK], BF16, name="v_grouped%d" % h, align_bytes=64)
+            nc.scalar.copy(
+                grouped[:].bitcast(F32).rearrange("p (j m u) -> p j m u", j=2, u=2),
+                bank[:].rearrange("p (j u m) -> p j m u", j=2, u=2),
+            )
+            v_grouped.append(grouped)
+
+        def quant_vals(h):
+            codes = sb.tile([P, 2 * P], U32, name="v_codes%d" % h, tag="hold%d" % h, align_bytes=64)
+            scales = sb.tile([P, 2 * P], U8, name="v_scales%d" % h, align_bytes=64)
+            nc.vector.quantize_mx(out=codes[:].bitcast(FP8X4), scales=scales[:], in_=v_grouped[h][:])
+            v_codes.append(codes)
+            v_scales.append(scales)
+
+        rope_pair(0)
+        gather_vals(0)
+        gather_vals(1)
+        turn_vals(0)
+        rope_pair(1)
+
+        q_grouped = sb.tile([P, Q * PACK], BF16, name="q_grouped", align_bytes=64)
+        nc.scalar.copy(
+            q_grouped[:].rearrange("p (c i t) -> p c t i", i=4, t=PACK),
+            q_raw[:].rearrange("p (t c i) -> p c t i", i=4, t=PACK),
+        )
+        gather_vals(2)
+        gather_vals(3)
+
+        km = sb.tile([P, I * PACK], BF16, name="km", align_bytes=64)
+        nc.vector.tensor_tensor(
+            km[:].rearrange("p (c i t) -> p c t i", i=4, t=PACK),
+            cos_terms[:].rearrange("p (t c i) -> p c t i", i=4, t=PACK),
+            sin_terms[:].rearrange("p (t c i) -> p c t i", i=4, t=PACK),
+            ALU.add,
+        )
+        q_codes = sb.tile([P, Q], U32, name="q_codes", align_bytes=64)
+        q_scales = sb.tile([P, Q], U8, name="q_scales", align_bytes=64)
+        nc.vector.quantize_mx(out=q_codes[:].bitcast(FP8X4), scales=q_scales[:], in_=q_grouped[:])
+        k_codes = sb.tile([P, I], U32, name="k_codes", align_bytes=64)
+        k_scales = sb.tile([P, I], U8, name="k_scales", align_bytes=64)
+        nc.vector.quantize_mx(out=k_codes[:].bitcast(FP8X4), scales=k_scales[:], in_=km[:])
+
+        size_bank = ps.tile([P, I], F32, name="size_bank")
+        for r in range(PACK):
+            nc.tensor.transpose(size_bank[:, r * P : (r + 1) * P], size_col[:, r : r + 1].to_broadcast([P, P]), ident[:])
+
+        blocks = range(Q // P)
+        scores = []
+        for b in blocks:
+            sc = ps.tile([P, I], F32, name="scores%d" % b)
+            c = slice(b * P, (b + 1) * P)
+            nc.tensor.matmul_mx(
+                out=sc[:], lhsT=q_codes[:, c].bitcast(FP8X4), lhsT_scale=q_scales[:, c],
+                rhs=k_codes[:].bitcast(FP8X4), rhs_scale=k_scales[:], start=True, stop=True,
+            )
+            scores.append(sc)
+        quant_vals(0)
+        turn_vals(1)
+
+        probs, sums = [], []
+        for b in blocks:
+            neg_max = sb.tile([P, 1], F32, name="neg_max%d" % b)
+            nc.vector.tensor_reduce(neg_max[:], scores[b][:], AX.X, ALU.max, negate=True)
+            pr = sb.tile([P, I], F32, name="prob%d" % b, tag="hold%d" % (2 - b), align_bytes=64)
+            sm = sb.tile([P, 1], F32, name="sum%d" % b)
+            nc.scalar.activation(pr[:], scores[b][:], ACT.Exp, bias=neg_max[:], accum_out=sm[:])
+            probs.append(pr)
+            sums.append(sm)
+
+        w_grouped = []
+        for b in blocks:
+            inv = sb.tile([P, 1], F32, name="inv%d" % b)
+            nc.vector.reciprocal(inv[:], sums[b][:])
+            w = sb.tile([P, I], BF16, name="w%d" % b)
+            nc.vector.scalar_tensor_tensor(
+                w[:].rearrange("p (s r) -> p s r", r=PACK),
+                probs[b][:].rearrange("p (s r) -> p s r", r=PACK),
+                inv[:],
+                size_bank[:].rearrange("p (r s) -> p s r", r=PACK),
+                ALU.mult, ALU.mult,
+            )
+            bank = ps.tile([P, 2 * P], F32, name="wt_bank%d" % b)
+            words = w[:].bitcast(F32)
+            for u in range(2):
+                nc.tensor.transpose(bank[:, u * P : (u + 1) * P], words[:, u : I // 2 : 2], ident[:])
+            grouped = sb.tile([P, P * PACK], BF16, name="w_grouped%d" % b, tag="late%d" % (1 - b), align_bytes=64)
+            nc.scalar.copy(
+                grouped[:].bitcast(F32).rearrange("p (m u) -> p m u", u=2),
+                bank[:].rearrange("p (u m) -> p m u", u=2),
+            )
+            w_grouped.append(grouped)
+        quant_vals(1)
+
+        res = sb.tile([P, PACK * X], F32, name="res")
+        outs = []
+        for b in blocks:
+            w_codes = sb.tile([P, P], U32, name="w_codes%d" % b, align_bytes=64)
+            w_scales = sb.tile([P, P], U8, name="w_scales%d" % b, align_bytes=64)
+            nc.vector.quantize_mx(out=w_codes[:].bitcast(FP8X4), scales=w_scales[:], in_=w_grouped[b][:])
+            o_bank = ps.tile([P, PACK * P], F32, name="o_bank%d" % b, tag="vo%d" % b)
+            for j in range(PACK):
+                c = slice(j * P, (j + 1) * P)
+                vc = slice(j % 2 * P, (j % 2 + 1) * P)
+                nc.tensor.matmul_mx(
+                    out=o_bank[:, c], lhsT=v_codes[j // 2][:, vc].bitcast(FP8X4), lhsT_scale=v_scales[j // 2][:, vc],
+                    rhs=w_codes[:].bitcast(FP8X4), rhs_scale=w_scales[:], start=True, stop=True,
+                )
+            outs.append(o_bank)
+        xs = P // HEADS
+        obs = []
+        for b in blocks:
+            ob = sb.tile([P, PACK * P], F32, name="ob%d" % b, tag="late%d" % b, align_bytes=64)
+            obs.append(ob)
+            nc.vector.tensor_tensor(
+                ob[:].rearrange("p (j q) -> p j q", j=PACK),
+                outs[b][:].rearrange("p (j q) -> p j q", j=PACK),
+                own_sb[:].rearrange("p (j q) -> p j q", j=PACK)[:, :, b * P : (b + 1) * P],
+                ALU.mult,
+            )
+        for b in blocks:
+            nc.vector.tensor_reduce(
+                res[:].rearrange("p (j x) -> p j x", j=PACK)[:, :, b * xs : (b + 1) * xs],
+                obs[b][:].rearrange("p (j x h) -> p j x h", j=PACK, h=HEADS),
+                AX.X, ALU.add,
+            )
+        nc.sync.dma_start(out=out.rearrange("(p j) x -> p (j x)", j=PACK), in_=res[:])

@@ -50,11 +50,11 @@ def tile_attend_ownlists_rope_kernel(tc, query, keys, cosn, sinn, size, vals, ow
         load(k_win[1][:], plane(keys, 1))
         load(s_win[0][:], plane(sinn, 0))
         load(v_raw[0][:], plane(vals, 0))
-        load(v_raw[1][:], plane(vals, 1))
         load(k_win[2][:], plane(keys, 2))
         load(c_win[1][:], plane(cosn, 2))
         load(k_win[3][:], plane(keys, 3))
         load(s_win[1][:], plane(sinn, 2))
+        load(v_raw[1][:], plane(vals, 1))
         load(q_raw[:], query.rearrange("(p t) q -> p (t q)", t=PACK))
         load(v_raw[2][:], plane(vals, 2))
         load(v_raw[3][:], plane(vals, 3))
@@ -64,7 +64,7 @@ def tile_attend_ownlists_rope_kernel(tc, query, keys, cosn, sinn, size, vals, ow
         ident = sb.tile([P, P], F32, name="ident")
         make_identity(nc, ident[:])
 
-        cos_terms = sb.tile([P, PACK * I], F32, name="cos_terms", tag="hold0", align_bytes=64)
+        cos_terms = sb.tile([P, PACK * I], F32, name="cos_terms")
         sin_terms = sb.tile([P, PACK * I], F32, name="sin_terms")
 
         def cols(t, n=1):
@@ -78,14 +78,11 @@ def tile_attend_ownlists_rope_kernel(tc, query, keys, cosn, sinn, size, vals, ow
             nc.vector.tensor_copy(cg[:], c_win[g][:].indirect(pos[:]))
             nc.vector.tensor_copy(kg[:, cols(1)], k_win[2 * g + 1][:].indirect(tok[:]))
             nc.vector.tensor_copy(sg[:], s_win[g][:].indirect(pos[:]))
-            nc.vector.tensor_tensor(
-                cos_terms[:, cols(2 * g, 2)].rearrange("p (t i) -> p t i", t=2),
-                kg[:].rearrange("p (t i) -> p t i", t=2),
-                cg[:].unsqueeze(1).to_broadcast([P, 2, I]),
-                ALU.mult,
-            )
+            for t in range(2):
+                nc.gpsimd.tensor_tensor(cos_terms[:, cols(2 * g + t)], kg[:, cols(t)], cg[:], ALU.mult)
             nc.vector.scalar_tensor_tensor(sin_terms[:, cols(2 * g)], kg[:, cols(1)], -1.0, sg[:], ALU.mult, ALU.mult)
-            nc.vector.tensor_tensor(sin_terms[:, cols(2 * g + 1)], kg[:, cols(0)], sg[:], ALU.mult)
+            eng = nc.gpsimd if g == 0 else nc.vector
+            eng.tensor_tensor(sin_terms[:, cols(2 * g + 1)], kg[:, cols(0)], sg[:], ALU.mult)
 
         v_gath = []
 
@@ -121,9 +118,8 @@ def tile_attend_ownlists_rope_kernel(tc, query, keys, cosn, sinn, size, vals, ow
 
         rope_pair(0)
         gather_vals(0)
-        gather_vals(1)
-        turn_vals(0)
         rope_pair(1)
+        gather_vals(1)
 
         q_grouped = sb.tile([P, Q * PACK], BF16, name="q_grouped", align_bytes=64)
         nc.scalar.copy(
@@ -131,9 +127,8 @@ def tile_attend_ownlists_rope_kernel(tc, query, keys, cosn, sinn, size, vals, ow
             q_raw[:].rearrange("p (t c i) -> p c t i", i=4, t=PACK),
         )
         gather_vals(2)
-        gather_vals(3)
 
-        km = sb.tile([P, I * PACK], BF16, name="km", align_bytes=64)
+        km = sb.tile([P, I * PACK], BF16, name="km", tag="km", align_bytes=64)
         nc.vector.tensor_tensor(
             km[:].rearrange("p (c i t) -> p c t i", i=4, t=PACK),
             cos_terms[:].rearrange("p (t c i) -> p c t i", i=4, t=PACK),
@@ -161,23 +156,28 @@ def tile_attend_ownlists_rope_kernel(tc, query, keys, cosn, sinn, size, vals, ow
                 rhs=k_codes[:].bitcast(FP8X4), rhs_scale=k_scales[:], start=True, stop=True,
             )
             scores.append(sc)
-        quant_vals(0)
-        turn_vals(1)
+        vg3 = sb.tile([P, I], BF16, name="vg3", tag="km", align_bytes=64)
+        nc.vector.tensor_copy(vg3[:], v_raw[3][:].indirect(tok[:]))
+        v_gath.append(vg3)
 
         probs, sums = [], []
         for b in blocks:
-            neg_max = sb.tile([P, 1], F32, name="neg_max%d" % b)
+            neg_max = sb.tile([P, 1], F32, name="neg_max%d" % b, tag="hold%d" % (3 * b), align_bytes=64)
             nc.vector.tensor_reduce(neg_max[:], scores[b][:], AX.X, ALU.max, negate=True)
             pr = sb.tile([P, I], F32, name="prob%d" % b, tag="hold%d" % (2 - b), align_bytes=64)
             sm = sb.tile([P, 1], F32, name="sum%d" % b)
             nc.scalar.activation(pr[:], scores[b][:], ACT.Exp, bias=neg_max[:], accum_out=sm[:])
             probs.append(pr)
             sums.append(sm)
+        turn_vals(0)
+        turn_vals(1)
 
         w_grouped = []
         for b in blocks:
             inv = sb.tile([P, 1], F32, name="inv%d" % b)
             nc.vector.reciprocal(inv[:], sums[b][:])
+            if b == 0:
+                quant_vals(0)
             w = sb.tile([P, I], BF16, name="w%d" % b)
             nc.vector.scalar_tensor_tensor(
                 w[:].rearrange("p (s r) -> p s r", r=PACK),

@@ -123,16 +123,16 @@ def tile_attend_ownlists_rope_kernel(tc, query, keys, cosn, sinn, size, vals, ow
 
         q_grouped = sb.tile([P, Q * PACK], BF16, name="q_grouped", align_bytes=64)
         nc.scalar.copy(
-            q_grouped[:].rearrange("p (c i t) -> p c t i", i=4, t=PACK),
-            q_raw[:].rearrange("p (t c i) -> p c t i", i=4, t=PACK),
+            q_grouped[:].rearrange("p (c i t) -> p c t i", i=2, t=PACK),
+            q_raw[:].rearrange("p (t c i) -> p c t i", i=2, t=PACK),
         )
         gather_vals(2)
 
         km = sb.tile([P, I * PACK], BF16, name="km", tag="km", align_bytes=64)
         nc.vector.tensor_tensor(
-            km[:].rearrange("p (c i t) -> p c t i", i=4, t=PACK),
-            cos_terms[:].rearrange("p (t c i) -> p c t i", i=4, t=PACK),
-            sin_terms[:].rearrange("p (t c i) -> p c t i", i=4, t=PACK),
+            km[:].rearrange("p (c i t) -> p c t i", i=2, t=PACK),
+            cos_terms[:].rearrange("p (t c i) -> p c t i", i=2, t=PACK),
+            sin_terms[:].rearrange("p (t c i) -> p c t i", i=2, t=PACK),
             ALU.add,
         )
         q_codes = sb.tile([P, Q], U32, name="q_codes", align_bytes=64)
@@ -179,17 +179,17 @@ def tile_attend_ownlists_rope_kernel(tc, query, keys, cosn, sinn, size, vals, ow
             if b == 0:
                 quant_vals(0)
             w = sb.tile([P, I], BF16, name="w%d" % b)
-            nc.vector.scalar_tensor_tensor(
-                w[:].rearrange("p (s r) -> p s r", r=PACK),
-                probs[b][:].rearrange("p (s r) -> p s r", r=PACK),
-                inv[:],
-                size_bank[:].rearrange("p (r s) -> p s r", r=PACK),
-                ALU.mult, ALU.mult,
-            )
             bank = ps.tile([P, 2 * P], F32, name="wt_bank%d" % b)
-            words = w[:].bitcast(F32)
             for u in range(2):
-                nc.tensor.transpose(bank[:, u * P : (u + 1) * P], words[:, u : I // 2 : 2], ident[:])
+                half = w[:, u * 2 * P : (u + 1) * 2 * P]
+                nc.vector.scalar_tensor_tensor(
+                    half.rearrange("p (s h) -> p s h", h=2),
+                    probs[b][:].rearrange("p (s u h) -> p u s h", u=2, h=2)[:, u],
+                    inv[:],
+                    size_bank[:].rearrange("p (u h s) -> p u s h", u=2, h=2)[:, u],
+                    ALU.mult, ALU.mult,
+                )
+                nc.tensor.transpose(bank[:, u * P : (u + 1) * P], half.bitcast(F32), ident[:])
             grouped = sb.tile([P, P * PACK], BF16, name="w_grouped%d" % b, tag="late%d" % (1 - b), align_bytes=64)
             nc.scalar.copy(
                 grouped[:].bitcast(F32).rearrange("p (m u) -> p m u", u=2),

@@ -49,9 +49,9 @@ def tile_attend_ownlists_rope_kernel(tc, query, keys, cosn, sinn, size, vals, ow
         load(pos[:], offs2)
         load(k_win[1][:], plane(keys, 1))
         load(s_win[0][:], plane(sinn, 0))
-        load(v_raw[0][:], plane(vals, 0))
         load(k_win[2][:], plane(keys, 2))
         load(c_win[1][:], plane(cosn, 2))
+        load(v_raw[0][:], plane(vals, 0))
         load(k_win[3][:], plane(keys, 3))
         load(s_win[1][:], plane(sinn, 2))
         load(v_raw[1][:], plane(vals, 1))
@@ -71,18 +71,23 @@ def tile_attend_ownlists_rope_kernel(tc, query, keys, cosn, sinn, size, vals, ow
             return slice(t * I, (t + n) * I)
 
         def rope_pair(g):
-            kg = sb.tile([P, 2 * I], F32, name="kg%d" % g)
+            kg = sb.tile([P, 3 * I], F32, name="kg%d" % g)
             cg = sb.tile([P, I], F32, name="cg%d" % g)
             sg = sb.tile([P, I], F32, name="sg%d" % g)
-            nc.vector.tensor_copy(kg[:, cols(0)], k_win[2 * g][:].indirect(tok[:]))
+            nc.vector.tensor_copy(kg[:, cols(1)], k_win[2 * g][:].indirect(tok[:]))
             nc.vector.tensor_copy(cg[:], c_win[g][:].indirect(pos[:]))
-            nc.vector.tensor_copy(kg[:, cols(1)], k_win[2 * g + 1][:].indirect(tok[:]))
+            nc.vector.tensor_copy(kg[:, cols(2)], k_win[2 * g + 1][:].indirect(tok[:]))
             nc.vector.tensor_copy(sg[:], s_win[g][:].indirect(pos[:]))
+            nc.scalar.activation(kg[:, cols(0)], kg[:, cols(2)], ACT.Copy, scale=-1.0)
             for t in range(2):
-                nc.gpsimd.tensor_tensor(cos_terms[:, cols(2 * g + t)], kg[:, cols(t)], cg[:], ALU.mult)
-            nc.vector.scalar_tensor_tensor(sin_terms[:, cols(2 * g)], kg[:, cols(1)], -1.0, sg[:], ALU.mult, ALU.mult)
+                nc.gpsimd.tensor_tensor(cos_terms[:, cols(2 * g + t)], kg[:, cols(1 + t)], cg[:], ALU.mult)
             eng = nc.gpsimd if g == 0 else nc.vector
-            eng.tensor_tensor(sin_terms[:, cols(2 * g + 1)], kg[:, cols(0)], sg[:], ALU.mult)
+            eng.tensor_tensor(
+                sin_terms[:, cols(2 * g, 2)].rearrange("p (t i) -> p t i", t=2),
+                kg[:, cols(0, 2)].rearrange("p (t i) -> p t i", t=2),
+                sg[:].unsqueeze(1).to_broadcast([P, 2, I]),
+                ALU.mult,
+            )
 
         v_gath = []
 
@@ -98,11 +103,11 @@ def tile_attend_ownlists_rope_kernel(tc, query, keys, cosn, sinn, size, vals, ow
 
         def turn_vals(h):
             bank = ps.tile([P, 4 * P], F32, name="vt_bank%d" % h, tag="vo%d" % h)
-            for j in range(2):
+            for j in (1, 0):
                 words = v_gath[2 * h + j][:].bitcast(F32)
                 for u in range(2):
                     nc.tensor.transpose(bank[:, (2 * j + u) * P : (2 * j + u + 1) * P], words[:, u : I // 2 : 2], ident[:])
-            grouped = sb.tile([P, 2 * P * PACK], BF16, name="v_grouped%d" % h, align_bytes=64)
+            grouped = sb.tile([P, 2 * P * PACK], BF16, name="v_grouped%d" % h, tag="hold%d" % (4 - h), align_bytes=64)
             nc.scalar.copy(
                 grouped[:].bitcast(F32).rearrange("p (j m u) -> p j m u", j=2, u=2),
                 bank[:].rearrange("p (j u m) -> p j m u", j=2, u=2),
@@ -172,31 +177,40 @@ def tile_attend_ownlists_rope_kernel(tc, query, keys, cosn, sinn, size, vals, ow
         turn_vals(0)
         turn_vals(1)
 
+        invs = [sb.tile([P, 1], F32, name="inv%d" % b) for b in blocks]
+        ws = [sb.tile([P, I], BF16, name="w%d" % b) for b in blocks]
+        wt_banks = [ps.tile([P, 2 * P], F32, name="wt_bank%d" % b) for b in blocks]
+
+        def weigh(b, u):
+            half = ws[b][:, u * 2 * P : (u + 1) * 2 * P]
+            nc.vector.scalar_tensor_tensor(
+                half.rearrange("p (s h) -> p s h", h=2),
+                probs[b][:].rearrange("p (s u h) -> p u s h", u=2, h=2)[:, u],
+                invs[b][:],
+                size_bank[:].rearrange("p (u h s) -> p u s h", u=2, h=2)[:, u],
+                ALU.mult, ALU.mult,
+            )
+            nc.tensor.transpose(wt_banks[b][:, u * P : (u + 1) * P], half.bitcast(F32), ident[:])
+
         w_grouped = []
-        for b in blocks:
-            inv = sb.tile([P, 1], F32, name="inv%d" % b)
-            nc.vector.reciprocal(inv[:], sums[b][:])
-            if b == 0:
-                quant_vals(0)
-            w = sb.tile([P, I], BF16, name="w%d" % b)
-            bank = ps.tile([P, 2 * P], F32, name="wt_bank%d" % b)
-            for u in range(2):
-                half = w[:, u * 2 * P : (u + 1) * 2 * P]
-                nc.vector.scalar_tensor_tensor(
-                    half.rearrange("p (s h) -> p s h", h=2),
-                    probs[b][:].rearrange("p (s u h) -> p u s h", u=2, h=2)[:, u],
-                    inv[:],
-                    size_bank[:].rearrange("p (u h s) -> p u s h", u=2, h=2)[:, u],
-                    ALU.mult, ALU.mult,
-                )
-                nc.tensor.transpose(bank[:, u * P : (u + 1) * P], half.bitcast(F32), ident[:])
+
+        def group_weights(b):
             grouped = sb.tile([P, P * PACK], BF16, name="w_grouped%d" % b, tag="late%d" % (1 - b), align_bytes=64)
             nc.scalar.copy(
                 grouped[:].bitcast(F32).rearrange("p (m u) -> p m u", u=2),
-                bank[:].rearrange("p (u m) -> p m u", u=2),
+                wt_banks[b][:].rearrange("p (u m) -> p m u", u=2),
             )
             w_grouped.append(grouped)
-        quant_vals(1)
+
+        nc.vector.reciprocal(invs[0][:], sums[0][:])
+        quant_vals(0)
+        weigh(0, 0)
+        nc.vector.reciprocal(invs[1][:], sums[1][:])
+        weigh(0, 1)
+        group_weights(0)
+        weigh(1, 0)
+        weigh(1, 1)
+        group_weights(1)
 
         res = sb.tile([P, PACK * X], F32, name="res")
         outs = []
@@ -204,6 +218,8 @@ def tile_attend_ownlists_rope_kernel(tc, query, keys, cosn, sinn, size, vals, ow
             w_codes = sb.tile([P, P], U32, name="w_codes%d" % b, align_bytes=64)
             w_scales = sb.tile([P, P], U8, name="w_scales%d" % b, align_bytes=64)
             nc.vector.quantize_mx(out=w_codes[:].bitcast(FP8X4), scales=w_scales[:], in_=w_grouped[b][:])
+            if b == 0:
+                quant_vals(1)
             o_bank = ps.tile([P, PACK * P], F32, name="o_bank%d" % b, tag="vo%d" % b)
             for j in range(PACK):
                 c = slice(j * P, (j + 1) * P)

@@ -17,8 +17,12 @@ P = 128
 PACK = 4
 D, T, I, Q, X, E = 512, 1024, 512, 256, 32, 512
 HEADS = Q // X
+LIST_COLS = I // 16
+RUN = 2
+MX_ALIGN = 64
+
 FLOPS = 2 * D * Q * I + 2 * I * E * Q
-BYTES = 4 * (D * Q + D * T + D * T + I + E * T + E * Q + E * X) + 2 * 2 * P * (I // 16)
+BYTES = 4 * (D * Q + D * T + D * T + I + E * T + E * Q + E * X) + 2 * 2 * P * LIST_COLS
 
 
 def tile_attend_ownlists_rope_kernel(tc, query, keys, cosn, sinn, size, vals, own, offs, offs2, out):
@@ -30,36 +34,57 @@ def tile_attend_ownlists_rope_kernel(tc, query, keys, cosn, sinn, size, vals, ow
         def plane(src, t):
             return src.rearrange("(p t) c -> p t c", t=PACK)[:, t, :]
 
-        tok = sb.tile([P, I // 16], U16, name="tok")
-        pos = sb.tile([P, I // 16], U16, name="pos")
+        def part(n, count=1):
+            return slice(n * I, (n + count) * I)
+
+        def quantise(name, values, codes_tag=""):
+            width = values.shape[1] // PACK
+            codes = sb.tile([P, width], U32, name=name + "_codes", tag=codes_tag, align_bytes=MX_ALIGN)
+            scales = sb.tile([P, width], U8, name=name + "_scales", align_bytes=MX_ALIGN)
+            nc.vector.quantize_mx(out=codes[:].bitcast(FP8X4), scales=scales[:], in_=values)
+            return codes, scales
+
+        def product(acc, stationary, columns, moving):
+            nc.tensor.matmul_mx(
+                out=acc,
+                lhsT=stationary[0][:, columns].bitcast(FP8X4),
+                lhsT_scale=stationary[1][:, columns],
+                rhs=moving[0][:].bitcast(FP8X4),
+                rhs_scale=moving[1][:],
+                start=True,
+                stop=True,
+            )
+
+        tokens = sb.tile([P, LIST_COLS], U16, name="tokens")
+        positions = sb.tile([P, LIST_COLS], U16, name="positions")
         k_win = [sb.tile([P, T], F32, name="k_win%d" % t) for t in range(PACK)]
-        c_win = [sb.tile([P, T], F32, name="c_win%d" % g) for g in range(2)]
-        s_win = [sb.tile([P, T], F32, name="s_win%d" % g) for g in range(2)]
+        cos_win = [sb.tile([P, T], F32, name="cos_win%d" % g) for g in range(2)]
+        sin_win = [sb.tile([P, T], F32, name="sin_win%d" % g) for g in range(2)]
         v_raw = [sb.tile([P, T], F32, name="v_raw%d" % t) for t in range(PACK)]
         q_raw = sb.tile([P, PACK * Q], F32, name="q_raw")
         own_sb = sb.tile([P, PACK * Q], F32, name="own_sb")
-        size_col = sb.tile([P, PACK], F32, name="size_col")
+        size_rows = sb.tile([P, PACK], F32, name="size_rows")
 
-        def load(dst, src):
-            nc.sync.dma_start(out=dst, in_=src)
-
-        load(k_win[0][:], plane(keys, 0))
-        load(tok[:], offs)
-        load(c_win[0][:], plane(cosn, 0))
-        load(pos[:], offs2)
-        load(k_win[1][:], plane(keys, 1))
-        load(s_win[0][:], plane(sinn, 0))
-        load(k_win[2][:], plane(keys, 2))
-        load(c_win[1][:], plane(cosn, 2))
-        load(v_raw[0][:], plane(vals, 0))
-        load(k_win[3][:], plane(keys, 3))
-        load(s_win[1][:], plane(sinn, 2))
-        load(v_raw[1][:], plane(vals, 1))
-        load(q_raw[:], query.rearrange("(p t) q -> p (t q)", t=PACK))
-        load(v_raw[2][:], plane(vals, 2))
-        load(v_raw[3][:], plane(vals, 3))
-        load(size_col[:], size.rearrange("o (s r) -> (o s) r", r=PACK))
-        load(own_sb[:], own.rearrange("(p t) q -> p (t q)", t=PACK))
+        for dst, src in (
+            (k_win[0], plane(keys, 0)),
+            (tokens, offs),
+            (cos_win[0], plane(cosn, 0)),
+            (positions, offs2),
+            (k_win[1], plane(keys, 1)),
+            (sin_win[0], plane(sinn, 0)),
+            (k_win[2], plane(keys, 2)),
+            (cos_win[1], plane(cosn, 2)),
+            (k_win[3], plane(keys, 3)),
+            (v_raw[0], plane(vals, 0)),
+            (sin_win[1], plane(sinn, 2)),
+            (v_raw[1], plane(vals, 1)),
+            (q_raw, query.rearrange("(p t) q -> p (t q)", t=PACK)),
+            (v_raw[2], plane(vals, 2)),
+            (v_raw[3], plane(vals, 3)),
+            (size_rows, size.rearrange("o (s r) -> (o s) r", r=PACK)),
+            (own_sb, own.rearrange("(p t) q -> p (t q)", t=PACK)),
+        ):
+            nc.sync.dma_start(out=dst[:], in_=src)
 
         ident = sb.tile([P, P], F32, name="ident")
         make_identity(nc, ident[:])
@@ -67,183 +92,165 @@ def tile_attend_ownlists_rope_kernel(tc, query, keys, cosn, sinn, size, vals, ow
         cos_terms = sb.tile([P, PACK * I], F32, name="cos_terms")
         sin_terms = sb.tile([P, PACK * I], F32, name="sin_terms")
 
-        def cols(t, n=1):
-            return slice(t * I, (t + n) * I)
+        def gather_pair(g, even, odd):
+            cos_g = sb.tile([P, I], F32, name="cos_g%d" % g)
+            sin_g = sb.tile([P, I], F32, name="sin_g%d" % g)
+            nc.vector.tensor_copy(even, k_win[2 * g][:].indirect(tokens[:]))
+            nc.vector.tensor_copy(cos_g[:], cos_win[g][:].indirect(positions[:]))
+            nc.vector.tensor_copy(odd, k_win[2 * g + 1][:].indirect(tokens[:]))
+            nc.vector.tensor_copy(sin_g[:], sin_win[g][:].indirect(positions[:]))
+            nc.gpsimd.tensor_tensor(cos_terms[:, part(2 * g)], even, cos_g[:], ALU.mult)
+            nc.gpsimd.tensor_tensor(cos_terms[:, part(2 * g + 1)], odd, cos_g[:], ALU.mult)
+            return sin_g
 
-        def rope_pair(g):
-            kg = sb.tile([P, 3 * I], F32, name="kg%d" % g)
-            cg = sb.tile([P, I], F32, name="cg%d" % g)
-            sg = sb.tile([P, I], F32, name="sg%d" % g)
-            nc.vector.tensor_copy(kg[:, cols(1)], k_win[2 * g][:].indirect(tok[:]))
-            nc.vector.tensor_copy(cg[:], c_win[g][:].indirect(pos[:]))
-            nc.vector.tensor_copy(kg[:, cols(2)], k_win[2 * g + 1][:].indirect(tok[:]))
-            nc.vector.tensor_copy(sg[:], s_win[g][:].indirect(pos[:]))
-            nc.scalar.activation(kg[:, cols(0)], kg[:, cols(2)], ACT.Copy, scale=-1.0)
-            for t in range(2):
-                nc.gpsimd.tensor_tensor(cos_terms[:, cols(2 * g + t)], kg[:, cols(1 + t)], cg[:], ALU.mult)
-            eng = nc.gpsimd if g == 0 else nc.vector
-            eng.tensor_tensor(
-                sin_terms[:, cols(2 * g, 2)].rearrange("p (t i) -> p t i", t=2),
-                kg[:, cols(0, 2)].rearrange("p (t i) -> p t i", t=2),
-                sg[:].unsqueeze(1).to_broadcast([P, 2, I]),
-                ALU.mult,
-            )
+        v_gathered = []
 
-        v_gath = []
-
-        def gather_vals(t):
+        def gather_vals_on_scalar(t):
             v_win = sb.tile([P, T], BF16, name="v_win%d" % t)
-            vg = sb.tile([P, I], BF16, name="vg%d" % t)
+            gathered = sb.tile([P, I], BF16, name="v_gathered%d" % t)
             nc.scalar.activation(v_win[:], v_raw[t][:], ACT.Copy)
-            nc.scalar.activation(vg[:], v_win[:].indirect(tok[:]), ACT.Copy)
-            v_gath.append(vg)
+            nc.scalar.activation(gathered[:], v_win[:].indirect(tokens[:]), ACT.Copy)
+            v_gathered.append(gathered)
 
-        v_codes, v_scales = [], []
-        v_grouped = []
+        first_keys = sb.tile([P, 3 * I], F32, name="first_keys")
+        first_sin = gather_pair(0, first_keys[:, part(1)], first_keys[:, part(2)])
+        nc.scalar.activation(first_keys[:, part(0)], first_keys[:, part(2)], ACT.Copy, scale=-1.0)
+        nc.gpsimd.tensor_tensor(
+            sin_terms[:, part(0, 2)].rearrange("p (t i) -> p t i", t=2),
+            first_keys[:, part(0, 2)].rearrange("p (t i) -> p t i", t=2),
+            first_sin[:].unsqueeze(1).to_broadcast([P, 2, I]),
+            ALU.mult,
+        )
+        gather_vals_on_scalar(0)
 
-        def turn_vals(h):
-            bank = ps.tile([P, 4 * P], F32, name="vt_bank%d" % h, tag="vo%d" % h)
-            for j in (1, 0):
-                words = v_gath[2 * h + j][:].bitcast(F32)
+        second_keys = sb.tile([P, 2 * I], F32, name="second_keys")
+        even, odd = second_keys[:, part(0)], second_keys[:, part(1)]
+        second_sin = gather_pair(1, even, odd)
+        nc.vector.scalar_tensor_tensor(sin_terms[:, part(2)], odd, -1.0, second_sin[:], ALU.mult, ALU.mult)
+        nc.vector.tensor_tensor(sin_terms[:, part(3)], even, second_sin[:], ALU.mult)
+        gather_vals_on_scalar(1)
+
+        q_grouped = sb.tile([P, Q * PACK], BF16, name="q_grouped", align_bytes=MX_ALIGN)
+        nc.scalar.copy(
+            q_grouped[:].rearrange("p (c n t) -> p c t n", n=RUN, t=PACK),
+            q_raw[:].rearrange("p (t c n) -> p c t n", n=RUN, t=PACK),
+        )
+        gather_vals_on_scalar(2)
+
+        km = sb.tile([P, I * PACK], BF16, name="km", tag="km_then_v3", align_bytes=MX_ALIGN)
+        nc.vector.tensor_tensor(
+            km[:].rearrange("p (c n t) -> p c t n", n=RUN, t=PACK),
+            cos_terms[:].rearrange("p (t c n) -> p c t n", n=RUN, t=PACK),
+            sin_terms[:].rearrange("p (t c n) -> p c t n", n=RUN, t=PACK),
+            ALU.add,
+        )
+        q_mx = quantise("q", q_grouped[:])
+        k_mx = quantise("k", km[:])
+
+        size_bank = ps.tile([P, I], F32, name="size_bank")
+        for r in range(PACK):
+            nc.tensor.transpose(size_bank[:, r * P : (r + 1) * P], size_rows[:, r : r + 1].to_broadcast([P, P]), ident[:])
+
+        blocks = range(Q // P)
+        scores = [ps.tile([P, I], F32, name="scores%d" % b) for b in blocks]
+        for b in blocks:
+            product(scores[b][:], q_mx, slice(b * P, (b + 1) * P), k_mx)
+
+        last_gathered = sb.tile([P, I], BF16, name="v_gathered3", tag="km_then_v3", align_bytes=MX_ALIGN)
+        nc.vector.tensor_copy(last_gathered[:], v_raw[3][:].indirect(tokens[:]))
+        v_gathered.append(last_gathered)
+
+        max_tags = ("max0_then_v_codes0", "max1_then_v_grouped1")
+        prob_tags = ("prob0", "prob1_then_v_codes1")
+        probs, sums = [], []
+        for b in blocks:
+            neg_max = sb.tile([P, 1], F32, name="neg_max%d" % b, tag=max_tags[b], align_bytes=MX_ALIGN)
+            nc.vector.tensor_reduce(neg_max[:], scores[b][:], AX.X, ALU.max, negate=True)
+            prob = sb.tile([P, I], F32, name="prob%d" % b, tag=prob_tags[b], align_bytes=MX_ALIGN)
+            total = sb.tile([P, 1], F32, name="total%d" % b)
+            nc.scalar.activation(prob[:], scores[b][:], ACT.Exp, bias=neg_max[:], accum_out=total[:])
+            probs.append(prob)
+            sums.append(total)
+
+        def turn_vals(half, order, grouped_tag):
+            bank = ps.tile([P, 4 * P], F32, name="v_bank%d" % half, tag="v_then_o%d" % half)
+            for j in order:
+                words = v_gathered[2 * half + j][:].bitcast(F32)
                 for u in range(2):
                     nc.tensor.transpose(bank[:, (2 * j + u) * P : (2 * j + u + 1) * P], words[:, u : I // 2 : 2], ident[:])
-            grouped = sb.tile([P, 2 * P * PACK], BF16, name="v_grouped%d" % h, tag="hold%d" % (4 - h), align_bytes=64)
+            grouped = sb.tile([P, 2 * P * PACK], BF16, name="v_grouped%d" % half, tag=grouped_tag, align_bytes=MX_ALIGN)
             nc.scalar.copy(
                 grouped[:].bitcast(F32).rearrange("p (j m u) -> p j m u", j=2, u=2),
                 bank[:].rearrange("p (j u m) -> p j m u", j=2, u=2),
             )
-            v_grouped.append(grouped)
+            return grouped
 
-        def quant_vals(h):
-            codes = sb.tile([P, 2 * P], U32, name="v_codes%d" % h, tag="hold%d" % h, align_bytes=64)
-            scales = sb.tile([P, 2 * P], U8, name="v_scales%d" % h, align_bytes=64)
-            nc.vector.quantize_mx(out=codes[:].bitcast(FP8X4), scales=scales[:], in_=v_grouped[h][:])
-            v_codes.append(codes)
-            v_scales.append(scales)
+        v_grouped = [turn_vals(0, (0, 1), "v_grouped0"), turn_vals(1, (1, 0), max_tags[1])]
 
-        rope_pair(0)
-        gather_vals(0)
-        rope_pair(1)
-        gather_vals(1)
-
-        q_grouped = sb.tile([P, Q * PACK], BF16, name="q_grouped", align_bytes=64)
-        nc.scalar.copy(
-            q_grouped[:].rearrange("p (c i t) -> p c t i", i=2, t=PACK),
-            q_raw[:].rearrange("p (t c i) -> p c t i", i=2, t=PACK),
-        )
-        gather_vals(2)
-
-        km = sb.tile([P, I * PACK], BF16, name="km", tag="km", align_bytes=64)
-        nc.vector.tensor_tensor(
-            km[:].rearrange("p (c i t) -> p c t i", i=2, t=PACK),
-            cos_terms[:].rearrange("p (t c i) -> p c t i", i=2, t=PACK),
-            sin_terms[:].rearrange("p (t c i) -> p c t i", i=2, t=PACK),
-            ALU.add,
-        )
-        q_codes = sb.tile([P, Q], U32, name="q_codes", align_bytes=64)
-        q_scales = sb.tile([P, Q], U8, name="q_scales", align_bytes=64)
-        nc.vector.quantize_mx(out=q_codes[:].bitcast(FP8X4), scales=q_scales[:], in_=q_grouped[:])
-        k_codes = sb.tile([P, I], U32, name="k_codes", align_bytes=64)
-        k_scales = sb.tile([P, I], U8, name="k_scales", align_bytes=64)
-        nc.vector.quantize_mx(out=k_codes[:].bitcast(FP8X4), scales=k_scales[:], in_=km[:])
-
-        size_bank = ps.tile([P, I], F32, name="size_bank")
-        for r in range(PACK):
-            nc.tensor.transpose(size_bank[:, r * P : (r + 1) * P], size_col[:, r : r + 1].to_broadcast([P, P]), ident[:])
-
-        blocks = range(Q // P)
-        scores = []
-        for b in blocks:
-            sc = ps.tile([P, I], F32, name="scores%d" % b)
-            c = slice(b * P, (b + 1) * P)
-            nc.tensor.matmul_mx(
-                out=sc[:], lhsT=q_codes[:, c].bitcast(FP8X4), lhsT_scale=q_scales[:, c],
-                rhs=k_codes[:].bitcast(FP8X4), rhs_scale=k_scales[:], start=True, stop=True,
-            )
-            scores.append(sc)
-        vg3 = sb.tile([P, I], BF16, name="vg3", tag="km", align_bytes=64)
-        nc.vector.tensor_copy(vg3[:], v_raw[3][:].indirect(tok[:]))
-        v_gath.append(vg3)
-
-        probs, sums = [], []
-        for b in blocks:
-            neg_max = sb.tile([P, 1], F32, name="neg_max%d" % b, tag="hold%d" % (3 * b), align_bytes=64)
-            nc.vector.tensor_reduce(neg_max[:], scores[b][:], AX.X, ALU.max, negate=True)
-            pr = sb.tile([P, I], F32, name="prob%d" % b, tag="hold%d" % (2 - b), align_bytes=64)
-            sm = sb.tile([P, 1], F32, name="sum%d" % b)
-            nc.scalar.activation(pr[:], scores[b][:], ACT.Exp, bias=neg_max[:], accum_out=sm[:])
-            probs.append(pr)
-            sums.append(sm)
-        turn_vals(0)
-        turn_vals(1)
-
-        invs = [sb.tile([P, 1], F32, name="inv%d" % b) for b in blocks]
-        ws = [sb.tile([P, I], BF16, name="w%d" % b) for b in blocks]
-        wt_banks = [ps.tile([P, 2 * P], F32, name="wt_bank%d" % b) for b in blocks]
+        inverses = [sb.tile([P, 1], F32, name="inverse%d" % b) for b in blocks]
+        weights = [sb.tile([P, I], BF16, name="weights%d" % b) for b in blocks]
+        w_banks = [ps.tile([P, 2 * P], F32, name="w_bank%d" % b) for b in blocks]
 
         def weigh(b, u):
-            half = ws[b][:, u * 2 * P : (u + 1) * 2 * P]
+            words = weights[b][:, u * 2 * P : (u + 1) * 2 * P]
             nc.vector.scalar_tensor_tensor(
-                half.rearrange("p (s h) -> p s h", h=2),
+                words.rearrange("p (s h) -> p s h", h=2),
                 probs[b][:].rearrange("p (s u h) -> p u s h", u=2, h=2)[:, u],
-                invs[b][:],
+                inverses[b][:],
                 size_bank[:].rearrange("p (u h s) -> p u s h", u=2, h=2)[:, u],
-                ALU.mult, ALU.mult,
+                ALU.mult,
+                ALU.mult,
             )
-            nc.tensor.transpose(wt_banks[b][:, u * P : (u + 1) * P], half.bitcast(F32), ident[:])
+            nc.tensor.transpose(w_banks[b][:, u * P : (u + 1) * P], words.bitcast(F32), ident[:])
 
-        w_grouped = []
+        swap_tags = ("w_grouped0_then_masked1", "w_grouped1_then_masked0")
 
         def group_weights(b):
-            grouped = sb.tile([P, P * PACK], BF16, name="w_grouped%d" % b, tag="late%d" % (1 - b), align_bytes=64)
+            grouped = sb.tile([P, P * PACK], BF16, name="w_grouped%d" % b, tag=swap_tags[b], align_bytes=MX_ALIGN)
             nc.scalar.copy(
                 grouped[:].bitcast(F32).rearrange("p (m u) -> p m u", u=2),
-                wt_banks[b][:].rearrange("p (u m) -> p m u", u=2),
+                w_banks[b][:].rearrange("p (u m) -> p m u", u=2),
             )
-            w_grouped.append(grouped)
+            return grouped
 
-        nc.vector.reciprocal(invs[0][:], sums[0][:])
-        quant_vals(0)
+        nc.vector.reciprocal(inverses[0][:], sums[0][:])
+        v_mx = [quantise("v0", v_grouped[0][:], max_tags[0])]
         weigh(0, 0)
-        nc.vector.reciprocal(invs[1][:], sums[1][:])
+        nc.vector.reciprocal(inverses[1][:], sums[1][:])
         weigh(0, 1)
-        group_weights(0)
+        w_grouped = [group_weights(0)]
         weigh(1, 0)
         weigh(1, 1)
-        group_weights(1)
+        w_grouped.append(group_weights(1))
 
-        res = sb.tile([P, PACK * X], F32, name="res")
-        outs = []
-        for b in blocks:
-            w_codes = sb.tile([P, P], U32, name="w_codes%d" % b, align_bytes=64)
-            w_scales = sb.tile([P, P], U8, name="w_scales%d" % b, align_bytes=64)
-            nc.vector.quantize_mx(out=w_codes[:].bitcast(FP8X4), scales=w_scales[:], in_=w_grouped[b][:])
-            if b == 0:
-                quant_vals(1)
-            o_bank = ps.tile([P, PACK * P], F32, name="o_bank%d" % b, tag="vo%d" % b)
+        def values_times_weights(b, w_mx):
+            o_bank = ps.tile([P, PACK * P], F32, name="o_bank%d" % b, tag="v_then_o%d" % b)
             for j in range(PACK):
-                c = slice(j * P, (j + 1) * P)
-                vc = slice(j % 2 * P, (j % 2 + 1) * P)
-                nc.tensor.matmul_mx(
-                    out=o_bank[:, c], lhsT=v_codes[j // 2][:, vc].bitcast(FP8X4), lhsT_scale=v_scales[j // 2][:, vc],
-                    rhs=w_codes[:].bitcast(FP8X4), rhs_scale=w_scales[:], start=True, stop=True,
-                )
-            outs.append(o_bank)
-        xs = P // HEADS
-        obs = []
+                product(o_bank[:, j * P : (j + 1) * P], v_mx[j // 2], slice(j % 2 * P, (j % 2 + 1) * P), w_mx)
+            return o_bank
+
+        first_w_mx = quantise("w0", w_grouped[0][:])
+        v_mx.append(quantise("v1", v_grouped[1][:], prob_tags[1]))
+        o_banks = [values_times_weights(0, first_w_mx)]
+        o_banks.append(values_times_weights(1, quantise("w1", w_grouped[1][:])))
+
+        masked = []
         for b in blocks:
-            ob = sb.tile([P, PACK * P], F32, name="ob%d" % b, tag="late%d" % b, align_bytes=64)
-            obs.append(ob)
+            tile = sb.tile([P, PACK * P], F32, name="masked%d" % b, tag=swap_tags[1 - b], align_bytes=MX_ALIGN)
             nc.vector.tensor_tensor(
-                ob[:].rearrange("p (j q) -> p j q", j=PACK),
-                outs[b][:].rearrange("p (j q) -> p j q", j=PACK),
+                tile[:].rearrange("p (j q) -> p j q", j=PACK),
+                o_banks[b][:].rearrange("p (j q) -> p j q", j=PACK),
                 own_sb[:].rearrange("p (j q) -> p j q", j=PACK)[:, :, b * P : (b + 1) * P],
                 ALU.mult,
             )
+            masked.append(tile)
+        result = sb.tile([P, PACK * X], F32, name="result")
+        places = P // HEADS
         for b in blocks:
             nc.vector.tensor_reduce(
-                res[:].rearrange("p (j x) -> p j x", j=PACK)[:, :, b * xs : (b + 1) * xs],
-                obs[b][:].rearrange("p (j x h) -> p j x h", j=PACK, h=HEADS),
-                AX.X, ALU.add,
+                result[:].rearrange("p (j x) -> p j x", j=PACK)[:, :, b * places : (b + 1) * places],
+                masked[b][:].rearrange("p (j x h) -> p j x h", j=PACK, h=HEADS),
+                AX.X,
+                ALU.add,
             )
-        nc.sync.dma_start(out=out.rearrange("(p j) x -> p (j x)", j=PACK), in_=res[:])
+        nc.sync.dma_start(out=out.rearrange("(p j) x -> p (j x)", j=PACK), in_=result[:])

from contextlib import ExitStack

import concourse.mybir as mybir
from concourse.masks import make_identity

F32 = mybir.dt.float32
BF16 = mybir.dt.bfloat16
U32 = mybir.dt.uint32
U16 = mybir.dt.uint16
U8 = mybir.dt.uint8
FP8X4 = mybir.dt.float8_e4m3fn_x4
ALU = mybir.AluOpType
ACT = mybir.ActivationFunctionType
AX = mybir.AxisListType

P = 128
PACK = 4
D, T, I, Q, X, E = 512, 1024, 512, 256, 32, 512
HEADS = Q // X
LIST_COLS = I // 16
RUN = 2
MX_ALIGN = 64

FLOPS = 2 * D * Q * I + 2 * I * E * Q
BYTES = 4 * (D * Q + D * T + D * T + I + E * T + E * Q + E * X) + 2 * 2 * P * LIST_COLS


def tile_attend_ownlists_rope_kernel(tc, query, keys, cosn, sinn, size, vals, own, offs, offs2, out):
    nc = tc.nc
    with ExitStack() as ctx:
        sb = ctx.enter_context(tc.tile_pool(name="sb", bufs=1))
        ps = ctx.enter_context(tc.psum_pool(name="ps", bufs=1))

        def plane(src, t):
            return src.rearrange("(p t) c -> p t c", t=PACK)[:, t, :]

        def part(n, count=1):
            return slice(n * I, (n + count) * I)

        def quantise(name, values, codes_tag=""):
            width = values.shape[1] // PACK
            codes = sb.tile([P, width], U32, name=name + "_codes", tag=codes_tag, align_bytes=MX_ALIGN)
            scales = sb.tile([P, width], U8, name=name + "_scales", align_bytes=MX_ALIGN)
            nc.vector.quantize_mx(out=codes[:].bitcast(FP8X4), scales=scales[:], in_=values)
            return codes, scales

        def product(acc, stationary, columns, moving):
            nc.tensor.matmul_mx(
                out=acc,
                lhsT=stationary[0][:, columns].bitcast(FP8X4),
                lhsT_scale=stationary[1][:, columns],
                rhs=moving[0][:].bitcast(FP8X4),
                rhs_scale=moving[1][:],
                start=True,
                stop=True,
            )

        tokens = sb.tile([P, LIST_COLS], U16, name="tokens")
        positions = sb.tile([P, LIST_COLS], U16, name="positions")
        k_win = [sb.tile([P, T], F32, name="k_win%d" % t) for t in range(PACK)]
        cos_win = [sb.tile([P, T], F32, name="cos_win%d" % g) for g in range(2)]
        sin_win = [sb.tile([P, T], F32, name="sin_win%d" % g) for g in range(2)]
        v_raw = [sb.tile([P, T], F32, name="v_raw%d" % t) for t in range(PACK)]
        q_raw = sb.tile([P, PACK * Q], F32, name="q_raw")
        own_sb = sb.tile([P, PACK * Q], F32, name="own_sb")
        size_rows = sb.tile([P, PACK], F32, name="size_rows")

        for dst, src in (
            (k_win[0], plane(keys, 0)),
            (tokens, offs),
            (cos_win[0], plane(cosn, 0)),
            (positions, offs2),
            (k_win[1], plane(keys, 1)),
            (sin_win[0], plane(sinn, 0)),
            (k_win[2], plane(keys, 2)),
            (cos_win[1], plane(cosn, 2)),
            (k_win[3], plane(keys, 3)),
            (v_raw[0], plane(vals, 0)),
            (sin_win[1], plane(sinn, 2)),
            (v_raw[1], plane(vals, 1)),
            (q_raw, query.rearrange("(p t) q -> p (t q)", t=PACK)),
            (v_raw[2], plane(vals, 2)),
            (v_raw[3], plane(vals, 3)),
            (size_rows, size.rearrange("o (s r) -> (o s) r", r=PACK)),
            (own_sb, own.rearrange("(p t) q -> p (t q)", t=PACK)),
        ):
            nc.sync.dma_start(out=dst[:], in_=src)

        ident = sb.tile([P, P], F32, name="ident")
        make_identity(nc, ident[:])

        cos_terms = sb.tile([P, PACK * I], F32, name="cos_terms")
        sin_terms = sb.tile([P, PACK * I], F32, name="sin_terms")

        def gather_pair(g, even, odd):
            cos_g = sb.tile([P, I], F32, name="cos_g%d" % g)
            sin_g = sb.tile([P, I], F32, name="sin_g%d" % g)
            nc.vector.tensor_copy(even, k_win[2 * g][:].indirect(tokens[:]))
            nc.vector.tensor_copy(cos_g[:], cos_win[g][:].indirect(positions[:]))
            nc.vector.tensor_copy(odd, k_win[2 * g + 1][:].indirect(tokens[:]))
            nc.vector.tensor_copy(sin_g[:], sin_win[g][:].indirect(positions[:]))
            nc.gpsimd.tensor_tensor(cos_terms[:, part(2 * g)], even, cos_g[:], ALU.mult)
            nc.gpsimd.tensor_tensor(cos_terms[:, part(2 * g + 1)], odd, cos_g[:], ALU.mult)
            return sin_g

        v_gathered = []

        def gather_vals_on_scalar(t):
            v_win = sb.tile([P, T], BF16, name="v_win%d" % t)
            gathered = sb.tile([P, I], BF16, name="v_gathered%d" % t)
            nc.scalar.activation(v_win[:], v_raw[t][:], ACT.Copy)
            nc.scalar.activation(gathered[:], v_win[:].indirect(tokens[:]), ACT.Copy)
            v_gathered.append(gathered)

        first_keys = sb.tile([P, 3 * I], F32, name="first_keys")
        first_sin = gather_pair(0, first_keys[:, part(1)], first_keys[:, part(2)])
        nc.scalar.activation(first_keys[:, part(0)], first_keys[:, part(2)], ACT.Copy, scale=-1.0)
        nc.gpsimd.tensor_tensor(
            sin_terms[:, part(0, 2)].rearrange("p (t i) -> p t i", t=2),
            first_keys[:, part(0, 2)].rearrange("p (t i) -> p t i", t=2),
            first_sin[:].unsqueeze(1).to_broadcast([P, 2, I]),
            ALU.mult,
        )
        gather_vals_on_scalar(0)

        second_keys = sb.tile([P, 2 * I], F32, name="second_keys")
        even, odd = second_keys[:, part(0)], second_keys[:, part(1)]
        second_sin = gather_pair(1, even, odd)
        nc.vector.scalar_tensor_tensor(sin_terms[:, part(2)], odd, -1.0, second_sin[:], ALU.mult, ALU.mult)
        nc.vector.tensor_tensor(sin_terms[:, part(3)], even, second_sin[:], ALU.mult)
        gather_vals_on_scalar(1)

        q_grouped = sb.tile([P, Q * PACK], BF16, name="q_grouped", align_bytes=MX_ALIGN)
        nc.scalar.copy(
            q_grouped[:].rearrange("p (c n t) -> p c t n", n=RUN, t=PACK),
            q_raw[:].rearrange("p (t c n) -> p c t n", n=RUN, t=PACK),
        )
        gather_vals_on_scalar(2)

        km = sb.tile([P, I * PACK], BF16, name="km", tag="km_then_v3", align_bytes=MX_ALIGN)
        nc.vector.tensor_tensor(
            km[:].rearrange("p (c n t) -> p c t n", n=RUN, t=PACK),
            cos_terms[:].rearrange("p (t c n) -> p c t n", n=RUN, t=PACK),
            sin_terms[:].rearrange("p (t c n) -> p c t n", n=RUN, t=PACK),
            ALU.add,
        )
        q_mx = quantise("q", q_grouped[:])
        k_mx = quantise("k", km[:])

        size_bank = ps.tile([P, I], F32, name="size_bank")
        for r in range(PACK):
            nc.tensor.transpose(size_bank[:, r * P : (r + 1) * P], size_rows[:, r : r + 1].to_broadcast([P, P]), ident[:])

        blocks = range(Q // P)
        scores = [ps.tile([P, I], F32, name="scores%d" % b) for b in blocks]
        for b in blocks:
            product(scores[b][:], q_mx, slice(b * P, (b + 1) * P), k_mx)

        last_gathered = sb.tile([P, I], BF16, name="v_gathered3", tag="km_then_v3", align_bytes=MX_ALIGN)
        nc.vector.tensor_copy(last_gathered[:], v_raw[3][:].indirect(tokens[:]))
        v_gathered.append(last_gathered)

        max_tags = ("max0_then_v_codes0", "max1_then_v_grouped1")
        prob_tags = ("prob0", "prob1_then_v_codes1")
        probs, sums = [], []
        for b in blocks:
            neg_max = sb.tile([P, 1], F32, name="neg_max%d" % b, tag=max_tags[b], align_bytes=MX_ALIGN)
            nc.vector.tensor_reduce(neg_max[:], scores[b][:], AX.X, ALU.max, negate=True)
            prob = sb.tile([P, I], F32, name="prob%d" % b, tag=prob_tags[b], align_bytes=MX_ALIGN)
            total = sb.tile([P, 1], F32, name="total%d" % b)
            nc.scalar.activation(prob[:], scores[b][:], ACT.Exp, bias=neg_max[:], accum_out=total[:])
            probs.append(prob)
            sums.append(total)

        def turn_vals(half, order, grouped_tag):
            bank = ps.tile([P, 4 * P], F32, name="v_bank%d" % half, tag="v_then_o%d" % half)
            for j in order:
                words = v_gathered[2 * half + j][:].bitcast(F32)
                for u in range(2):
                    nc.tensor.transpose(bank[:, (2 * j + u) * P : (2 * j + u + 1) * P], words[:, u : I // 2 : 2], ident[:])
            grouped = sb.tile([P, 2 * P * PACK], BF16, name="v_grouped%d" % half, tag=grouped_tag, align_bytes=MX_ALIGN)
            nc.scalar.copy(
                grouped[:].bitcast(F32).rearrange("p (j m u) -> p j m u", j=2, u=2),
                bank[:].rearrange("p (j u m) -> p j m u", j=2, u=2),
            )
            return grouped

        v_grouped = [turn_vals(0, (0, 1), "v_grouped0"), turn_vals(1, (1, 0), max_tags[1])]

        inverses = [sb.tile([P, 1], F32, name="inverse%d" % b) for b in blocks]
        weights = [sb.tile([P, I], BF16, name="weights%d" % b) for b in blocks]
        w_banks = [ps.tile([P, 2 * P], F32, name="w_bank%d" % b) for b in blocks]

        def weigh(b, u):
            words = weights[b][:, u * 2 * P : (u + 1) * 2 * P]
            nc.vector.scalar_tensor_tensor(
                words.rearrange("p (s h) -> p s h", h=2),
                probs[b][:].rearrange("p (s u h) -> p u s h", u=2, h=2)[:, u],
                inverses[b][:],
                size_bank[:].rearrange("p (u h s) -> p u s h", u=2, h=2)[:, u],
                ALU.mult,
                ALU.mult,
            )
            nc.tensor.transpose(w_banks[b][:, u * P : (u + 1) * P], words.bitcast(F32), ident[:])

        swap_tags = ("w_grouped0_then_masked1", "w_grouped1_then_masked0")

        def group_weights(b):
            grouped = sb.tile([P, P * PACK], BF16, name="w_grouped%d" % b, tag=swap_tags[b], align_bytes=MX_ALIGN)
            nc.scalar.copy(
                grouped[:].bitcast(F32).rearrange("p (m u) -> p m u", u=2),
                w_banks[b][:].rearrange("p (u m) -> p m u", u=2),
            )
            return grouped

        nc.vector.reciprocal(inverses[0][:], sums[0][:])
        v_mx = [quantise("v0", v_grouped[0][:], max_tags[0])]
        weigh(0, 0)
        nc.vector.reciprocal(inverses[1][:], sums[1][:])
        weigh(0, 1)
        w_grouped = [group_weights(0)]
        weigh(1, 0)
        weigh(1, 1)
        w_grouped.append(group_weights(1))

        def values_times_weights(b, w_mx):
            o_bank = ps.tile([P, PACK * P], F32, name="o_bank%d" % b, tag="v_then_o%d" % b)
            for j in range(PACK):
                product(o_bank[:, j * P : (j + 1) * P], v_mx[j // 2], slice(j % 2 * P, (j % 2 + 1) * P), w_mx)
            return o_bank

        first_w_mx = quantise("w0", w_grouped[0][:])
        v_mx.append(quantise("v1", v_grouped[1][:], prob_tags[1]))
        o_banks = [values_times_weights(0, first_w_mx)]
        o_banks.append(values_times_weights(1, quantise("w1", w_grouped[1][:])))

        masked = []
        for b in blocks:
            tile = sb.tile([P, PACK * P], F32, name="masked%d" % b, tag=swap_tags[1 - b], align_bytes=MX_ALIGN)
            nc.vector.tensor_tensor(
                tile[:].rearrange("p (j q) -> p j q", j=PACK),
                o_banks[b][:].rearrange("p (j q) -> p j q", j=PACK),
                own_sb[:].rearrange("p (j q) -> p j q", j=PACK)[:, :, b * P : (b + 1) * P],
                ALU.mult,
            )
            masked.append(tile)
        result = sb.tile([P, PACK * X], F32, name="result")
        places = P // HEADS
        for b in blocks:
            nc.vector.tensor_reduce(
                result[:].rearrange("p (j x) -> p j x", j=PACK)[:, :, b * places : (b + 1) * places],
                masked[b][:].rearrange("p (j x h) -> p j x h", j=PACK, h=HEADS),
                AX.X,
                ALU.add,
            )
        nc.sync.dma_start(out=out.rearrange("(p j) x -> p (j x)", j=PACK), in_=result[:])
